import numpy as np
import ml_dtypes


def mxq(x, axis, fmt="e4m3"):
    dtype, down = {"e4m3": (ml_dtypes.float8_e4m3fn, 7), "e5m2": (ml_dtypes.float8_e5m2, 14)}[fmt]
    v = np.moveaxis(np.asarray(x, np.float32).astype(ml_dtypes.bfloat16).astype(np.float64), axis, -1)
    blocks = v.reshape(v.shape[:-1] + (-1, 32))
    amax = np.abs(blocks).max(-1, keepdims=True)
    byte = np.maximum(np.where(amax > 0, np.frexp(amax)[1] - 1 + 127, 0) - down, 1)
    scale = np.exp2(byte - 127.0)
    codes = (blocks / scale).astype(np.float32).astype(dtype).astype(np.float64)
    return np.moveaxis((codes * scale).reshape(v.shape), -1, axis)


WIDE = False


def mx_kscale(k):
    if not WIDE:
        return np.ones(k)
    levels = np.array([10, -10, 5, -5, 0])
    if k % 512:
        return np.exp2(np.random.permutation(np.resize(levels, k // 32))).repeat(32)
    a = np.empty((k // 512, 16))
    for p in range(k // 512):
        a[p, :8] = np.random.permutation(np.resize(levels, 8))
        for g in range(8):
            far = levels[np.abs(levels - a[p, g]) >= 10]
            a[p, g + 8] = far[np.random.randint(len(far))]
    return np.exp2(a.ravel()).repeat(32)


BF16 = ml_dtypes.bfloat16


def bf(x):
    return np.asarray(x, np.float32).astype(BF16)


def f64(x):
    return np.asarray(x).astype(np.float64)

def planes(Y):
    n, m = Y.shape
    b = f64(bf(Y)).reshape(n // 32, 32, m)
    amax = np.abs(b).max(1)
    byte = np.clip(np.where(amax > 0, np.frexp(amax)[1] - 1 + 127 - 7, 1), 1, 254)
    codes = (b * np.exp2(127.0 - byte)[:, None, :]).reshape(n, m).astype(np.float32).astype(ml_dtypes.float8_e4m3fn).view(np.uint8)
    words = codes.reshape(n // 512, 128, 4, m).transpose(0, 1, 3, 2)
    return np.ascontiguousarray(words), np.ascontiguousarray(byte.astype(np.uint8).reshape(n // 512, 16, m))


N, M, D = 1024, 1024, 512


def softmax(a, axis):
    e = np.exp(a - a.max(axis=axis, keepdims=True))
    return e / e.sum(axis=axis, keepdims=True)


def logsumexp(a, axis):
    top = a.max(axis=axis, keepdims=True)
    return top + np.log(np.exp(a - top).sum(axis=axis, keepdims=True))


def coupling_deviation(lt, u):
    m = lt.shape[1]
    return u[:, None] * (m * softmax(lt, 1) - 1.0)


def sinkhorn_sweep(s):
    n = s.shape[0]
    r = s - logsumexp(s, 1)
    return n * softmax(r, 0)


def setup_inputs():
    a, b, g = mx_kscale(N), mx_kscale(M), mx_kscale(D)
    lt = 0.7 * np.random.standard_normal((N, M)) + 0.5 * np.random.standard_normal((N, 1)) + 0.3 * np.random.standard_normal((1, M))
    return {
        "lt": bf(lt),
        "c1": bf(np.random.standard_normal((N, N)) / np.sqrt(N) / a[None, :]),
        "c2": bf(np.random.standard_normal((M, M)) / np.sqrt(M) / b[None, :]),
        "u": bf((1.0 + 0.2 * np.random.standard_normal(N)) * a),
        "v": bf((1.0 + 0.2 * np.random.standard_normal(M)) * b),
        "x": bf(np.random.standard_normal((N, D)) * g[None, :]),
        "y": bf(np.random.standard_normal((M, D)) / g[None, :]),
    }


def core(lt, c1, c2, u, v, x, y):
    lt = f64(lt)
    d = x.shape[1]
    t = coupling_deviation(lt, f64(u))
    ct = mxq(f64(c1), 1, "e4m3") @ mxq(t, 0, "e4m3")
    cv = ct * f64(v)[None, :]
    j = mxq(cv, 1, "e4m3") @ mxq(f64(c2), 1, "e4m3").T
    feat = (mxq(f64(x), 1, "e4m3") @ mxq(f64(y), 1, "e4m3").T) / np.sqrt(d)
    s = lt + 0.5 * j + 0.5 * feat
    return sinkhorn_sweep(s)


def reference(lt, c1, c2, u, v, x, y):
    R_out = core(lt, c1, c2, u, v, x, y)
    words, scales = planes(R_out)
    return R_out, words, scales

@@ -1,0 +1,427 @@
+from contextlib import ExitStack
+
+import concourse.mybir as mybir
+from concourse.masks import make_identity
+
+F32 = mybir.dt.float32
+BF16 = mybir.dt.bfloat16
+U32 = mybir.dt.uint32
+I32 = mybir.dt.int32
+U8 = mybir.dt.uint8
+FP8X4 = mybir.dt.float8_e4m3fn_x4
+ACT = mybir.ActivationFunctionType
+ALU = mybir.AluOpType
+AX = mybir.AxisListType
+
+P = 128
+N = 1024
+D = 512
+FLOPS = 2 * N * N * N * 2 + 2 * N * N * D
+
+LIFT = 72.0
+DEEP = 90.0
+W_SCALE = 2.0 ** 60
+
+C1_ENG = "ssssssss"
+X_ENG = "ssss"
+Y_ENG = "ssss"
+C2_ENG = "ssssssss"
+DD_EARLY = (0, 1, 2, 3)
+PLAN = "XXXXXXXX"
+CV_PLAN = "vggggggg"
+D_ENG = "v"
+
+
+def tile_bilinearcouplingupdatesinkhorn_kernel(tc, lt, c1, c2, u, v, x, y, out_0, out_1, out_2):
+    nc = tc.nc
+    with ExitStack() as ctx:
+        keep = ctx.enter_context(tc.tile_pool(name="keep", bufs=1))
+        rot = ctx.enter_context(tc.tile_pool(name="rot", bufs=2))
+        psum = ctx.enter_context(tc.psum_pool(name="psum", bufs=1))
+        ctx.enter_context(tc.manual_schedule())
+
+        lt_sb = [keep.tile([P, 4, N], BF16, name="lt%d" % g, align_bytes=64) for g in range(2)]
+        c1_sb = [keep.tile([P, 4, N], BF16, name="c1_%d" % g, align_bytes=64) for g in range(2)]
+        x_sb = keep.tile([P, 2, 4, D], BF16, name="x_sb", align_bytes=64)
+        y_sb = keep.tile([P, 8, D], BF16, name="y_sb", align_bytes=64)
+        c2_sb = keep.tile([P, 8, N], BF16, name="c2_sb", align_bytes=64)
+        u_raw = keep.tile([P, 2, 4], BF16, name="u_raw")
+        v_raw = keep.tile([P, 2, 4], BF16, name="v_raw")
+        for g in range(2):
+            rows = lt[512 * g : 512 * g + 512, :].rearrange("(p t) m -> p t m", t=4)
+            for tp in range(2):
+                nc.sync.dma_start(out=lt_sb[g][:, 2 * tp : 2 * tp + 2, :], in_=rows[:, 2 * tp : 2 * tp + 2, :])
+        nc.scalar.dma_start(out=u_raw[:], in_=u.rearrange("(g p t) -> p g t", p=P, t=4))
+        nc.scalar.dma_start(out=v_raw[:], in_=v.rearrange("(g p t) -> p g t", p=P, t=4))
+        for g in range(2):
+            nc.sync.dma_start(out=c1_sb[g][:], in_=c1[512 * g : 512 * g + 512, :].rearrange("(p t) m -> p t m", t=4))
+        nc.sync.dma_start(out=x_sb[:], in_=x.rearrange("(g p t) k -> p g t k", p=P, t=4))
+        nc.sync.dma_start(out=y_sb[:], in_=y.rearrange("(b p) k -> p b k", p=P))
+        for q in range(2):
+            nc.sync.dma_start(out=c2_sb[:, 4 * q : 4 * q + 4, :], in_=c2[512 * q : 512 * q + 512, :].rearrange("(b p) k -> p b k", p=P))
+
+        ident = keep.tile([P, P], F32, name="ident")
+        make_identity(nc, ident[:])
+        ident_n = keep.tile([P, P], F32, name="ident_n")
+        nc.gpsimd.tensor_scalar(out=ident_n[:], in0=ident[:], scalar1=float(N), scalar2=0.0, op0=ALU.mult, op1=ALU.add)
+        ident_b = keep.tile([P, P], BF16, name="ident_b")
+        make_identity(nc, ident_b[:])
+
+        u_f = keep.tile([P, 2, 4], F32, name="u_f")
+        v_f = keep.tile([P, 2, 4], F32, name="v_f")
+        mx = keep.tile([P, 8], F32, name="mx")
+        nmx = keep.tile([P, 8], F32, name="nmx")
+        rs = keep.tile([P, 8], F32, name="rs")
+        rrs = keep.tile([P, 8], F32, name="rrs")
+        amp = keep.tile([P, 8], F32, name="amp")
+        dd = keep.tile([P, 8, N], BF16, name="dd")
+        big = [keep.tile([P, 4, N], F32, name="big%d" % g) for g in range(2)]
+        t_codes = keep.tile([P, 2, N], U32, name="t_codes", align_bytes=64)
+        t_scales = keep.tile([P, 2, N], U8, name="t_scales", align_bytes=64)
+
+        def scratch(name, shape):
+            return rot.tile(shape, BF16, name=name, tag="grouped", align_bytes=64, bufs=5)
+
+        def quantize(codes, scales, grouped):
+            nc.vector.quantize_mx(out=codes.bitcast(FP8X4), scales=scales, in_=grouped)
+
+        def tree(qs):
+            level = {}
+            for q in qs:
+                g, tp = divmod(q, 2)
+                level[q] = lt_sb[g][:, 2 * tp : 2 * tp + 2, :]
+            width, lvl = N, 0
+            while width > 32:
+                half = width // 2
+                for q in qs:
+                    m = rot.tile([P, 2, half], BF16, name="m%d" % lvl, bufs=3)
+                    nc.vector.tensor_tensor(out=m[:], in0=level[q][:, :, 0:half], in1=level[q][:, :, half:width], op=ALU.max)
+                    level[q] = m[:]
+                width, lvl = half, lvl + 1
+            for q in qs:
+                nc.vector.tensor_reduce(out=mx[:, 2 * q : 2 * q + 2], in_=level[q], axis=AX.X, op=ALU.max)
+            s = slice(2 * qs[0], 2 * qs[-1] + 2)
+            nc.vector.tensor_scalar(out=nmx[:, s], in0=mx[:, s], scalar1=-1.0, scalar2=None, op0=ALU.mult)
+
+        def exps(q):
+            for s in (2 * q, 2 * q + 1):
+                g, t = divmod(s, 4)
+                nc.scalar.activation(out=big[g][:, t, :], in_=lt_sb[g][:, t, :], func=ACT.Exp, bias=nmx[:, s : s + 1],
+                                     scale=1.0, accum_out=rs[:, s : s + 1])
+
+        def depth(q):
+            for s in (2 * q, 2 * q + 1):
+                g, t = divmod(s, 4)
+                eng = nc.gpsimd if D_ENG == "g" else nc.vector
+                eng.tensor_scalar(out=dd[:, s, :], in0=lt_sb[g][:, t, :], scalar1=nmx[:, s : s + 1],
+                                  scalar2=1.0, op0=ALU.add, op1=ALU.mult)
+
+        tb = [scratch("tb%d" % g, [P, 4, N]) for g in range(2)]
+
+        def deviation(q):
+            g, tp = divmod(q, 2)
+            s = slice(2 * q, 2 * q + 2)
+            nc.vector.reciprocal(out=rrs[:, s], in_=rs[:, s])
+            nc.vector.scalar_tensor_tensor(out=amp[:, s], in0=rrs[:, s], scalar=float(N),
+                                           in1=u_f[:, g, 2 * tp : 2 * tp + 2], op0=ALU.mult, op1=ALU.mult)
+            for t in (2 * tp, 2 * tp + 1):
+                nc.vector.tensor_scalar(out=tb[g][:, t, :], in0=big[g][:, t, :], scalar1=amp[:, 4 * g + t : 4 * g + t + 1],
+                                        scalar2=u_f[:, g, t : t + 1], op0=ALU.mult, op1=ALU.subtract)
+
+        t_int = {}
+
+        def interleave_t(g, G, eng):
+            if g not in t_int:
+                t_int[g] = scratch("t_int", [P, N, 4])
+            o = t_int[g][:, 512 * G : 512 * G + 512, :].rearrange("p (T q) t -> p T q t", T=4)
+            i = tb[g][:, :, 512 * G : 512 * G + 512].rearrange("p t (q T) -> p T q t", T=4)
+            if eng == "v":
+                nc.vector.tensor_copy(out=o, in_=i)
+            else:
+                nc.scalar.copy(out=o, in_=i)
+
+        def quantize_t(g):
+            quantize(t_codes[:, g, :], t_scales[:, g, :], t_int[g][:].rearrange("p r j -> p (r j)"))
+
+        def turn_in(rows, pr, kappa, dst, eng):
+            dst_w = dst[:].rearrange("p r j -> p (r j)").bitcast(F32).rearrange("p (s r w) -> p s r w", s=8, w=2)
+            bank = psum.tile([P, 2, 2, P], F32, name="tp", bufs=3)
+            for s in range(2):
+                words = rows(2 * pr + s).bitcast(F32)
+                for w in range(2):
+                    nc.tensor.transpose(bank[:, s, w, :], words[:, 256 * kappa + w : 256 * kappa + 256 : 2], ident[:])
+            o = dst_w[:, 2 * pr : 2 * pr + 2, :, :]
+            i = bank[:].rearrange("p s w r -> p s r w")
+            if eng == "v":
+                nc.vector.tensor_copy(out=o, in_=i)
+            else:
+                nc.scalar.copy(out=o, in_=i)
+
+        def planes(name, kappas):
+            codes = keep.tile([P, kappas, N], U32, name=name + "_codes", align_bytes=64)
+            scales = keep.tile([P, kappas, N], U8, name=name + "_scales", align_bytes=64)
+            return codes, scales
+
+        def c1_rows(s):
+            return c1_sb[s // 4][:, s % 4, :]
+
+        def x_rows(s):
+            return x_sb[:, s // 4, s % 4, :]
+
+        def y_rows(s):
+            return y_sb[:, s, :]
+
+        def c2_rows(s):
+            return c2_sb[:, s, :]
+
+        c1_codes, c1_scales = planes("c1", 2)
+        x_codes, x_scales = planes("x", 1)
+        y_codes, y_scales = planes("y", 1)
+        c2_codes, c2_scales = planes("c2", 2)
+        feat_scale = 0.5 / (float(D) ** 0.5)
+
+        tree((0,))
+        exps(0)
+        tree((1,))
+        exps(1)
+        nc.vector.tensor_copy(out=u_f[:], in_=u_raw[:])
+        nc.vector.tensor_copy(out=v_f[:], in_=v_raw[:])
+        tree((2, 3))
+        exps(2)
+        exps(3)
+        deviation(0)
+        deviation(1)
+        c1_g = [scratch("c1_int", [P, N, 4]) for k in range(2)]
+
+        def turn_c1(half):
+            for k in range(2):
+                for pr in (2 * half, 2 * half + 1):
+                    turn_in(c1_rows, pr, k, c1_g[k], C1_ENG[4 * half + 2 * k + pr % 2])
+
+        turn_c1(0)
+        interleave_t(0, 0, "v")
+        interleave_t(0, 1, "s")
+        deviation(2)
+        deviation(3)
+        turn_c1(1)
+        interleave_t(1, 0, "v")
+        interleave_t(1, 1, "s")
+        for q in DD_EARLY:
+            depth(q)
+        quantize_t(0)
+        for k in range(2):
+            quantize(c1_codes[:, k, :], c1_scales[:, k, :], c1_g[k][:].rearrange("p r j -> p (r j)"))
+        quantize_t(1)
+
+        rmax = keep.tile([P, 8], F32, name="rmax")
+        nrmax = keep.tile([P, 8], F32, name="nrmax")
+        rs2 = keep.tile([P, 8], F32, name="rs2")
+        w1 = keep.tile([P, 8], F32, name="w1")
+        w2 = keep.tile([P, 8], F32, name="w2")
+        csum = keep.tile([P, 8], F32, name="csum")
+        cv = {}
+        jps = {}
+
+        def first_product(i):
+            cols = slice(P * i, P * i + P)
+            cv_int = rot.tile([P, 2, P, 4], BF16, name="cv_int", align_bytes=64, bufs=3)
+            cv_codes = rot.tile([P, 2, P], U32, name="cv_codes", align_bytes=64, bufs=3)
+            cv_scales = rot.tile([P, 2, P], U8, name="cv_scales", align_bytes=64, bufs=3)
+            cv[i] = (cv_int, cv_codes, cv_scales)
+            for G in range(2):
+                ctp = psum.tile([P, 4, P], F32, name="ctp", bufs=2)
+                for T in range(4):
+                    mcols = slice(512 * G + P * T, 512 * G + P * T + P)
+                    for k in range(2):
+                        nc.tensor.matmul_mx(out=ctp[:, T, :], lhsT=t_codes[:, k, mcols].bitcast(FP8X4), lhsT_scale=t_scales[:, k, mcols],
+                                            rhs=c1_codes[:, k, cols].bitcast(FP8X4), rhs_scale=c1_scales[:, k, cols],
+                                            start=(k == 0), stop=(k == 1))
+                if CV_PLAN[i] == "v":
+                    nc.vector.tensor_tensor(out=cv_int[:, G, :, :], in0=ctp[:].rearrange("p T i -> p i T"),
+                                            in1=v_f[:, G : G + 1, :].to_broadcast([P, P, 4]), op=ALU.mult)
+                else:
+                    flat = rot.tile([P, 4, P], BF16, name="cv_flat", bufs=4)
+                    for T in range(4):
+                        nc.scalar.activation(out=flat[:, T, :], in_=ctp[:, T, :], func=ACT.Copy, scale=v_f[:, G, T : T + 1])
+                    nc.gpsimd.tensor_scalar(out=cv_int[:, G, :, :], in0=flat[:].rearrange("p T i -> p i T"), scalar1=1.0, scalar2=0.0,
+                                            op0=ALU.mult, op1=ALU.add)
+
+        def quantize_cv(i):
+            cv_int, cv_codes, cv_scales = cv[i]
+            quantize(cv_codes[:].rearrange("p G i -> p (G i)"), cv_scales[:].rearrange("p G i -> p (G i)"),
+                     cv_int[:].rearrange("p G i T -> p (G i T)"))
+
+        def second_product(i):
+            cv_int, cv_codes, cv_scales = cv[i]
+            for h in range(2):
+                hc = slice(512 * h, 512 * h + 512)
+                jp = psum.tile([P, 512], F32, name="jp", bufs=2)
+                jps[i, h] = jp
+                for k in range(2):
+                    nc.tensor.matmul_mx(out=jp[:], lhsT=cv_codes[:, k, :].bitcast(FP8X4), lhsT_scale=cv_scales[:, k, :],
+                                        rhs=c2_codes[:, k, hc].bitcast(FP8X4), rhs_scale=c2_scales[:, k, hc],
+                                        start=(k == 0), stop=(k == 1))
+
+        def features(i):
+            g, t = divmod(i, 4)
+            cols = slice(P * i, P * i + P)
+            for h in range(2):
+                hc = slice(512 * h, 512 * h + 512)
+                dst = big[g][:, t, hc]
+                ft = psum.tile([P, 512], F32, name="tp", bufs=3)
+                nc.tensor.matmul_mx(out=ft[:], lhsT=x_codes[:, 0, cols].bitcast(FP8X4), lhsT_scale=x_scales[:, 0, cols],
+                                    rhs=y_codes[:, 0, hc].bitcast(FP8X4), rhs_scale=y_scales[:, 0, hc], start=True, stop=True)
+                if PLAN[i] == "Z":
+                    nc.vector.scalar_tensor_tensor(out=dst, in0=ft[:], scalar=feat_scale, in1=lt_sb[g][:, t, hc],
+                                                   op0=ALU.mult, op1=ALU.add)
+                    nc.gpsimd.tensor_tensor(out=dst, in0=dst, in1=guard[:, hc], op=ALU.subtract)
+                elif PLAN[i] == "X":
+                    nc.vector.scalar_tensor_tensor(out=dst, in0=ft[:], scalar=feat_scale, in1=guard[:, hc],
+                                                   op0=ALU.mult, op1=ALU.subtract)
+                    nc.gpsimd.tensor_tensor(out=dst, in0=dst, in1=lt_sb[g][:, t, hc], op=ALU.add)
+                else:
+                    nc.scalar.activation(out=dst, in_=ft[:], func=ACT.Copy, scale=feat_scale)
+                    nc.gpsimd.tensor_tensor(out=dst, in0=dst, in1=lt_sb[g][:, t, hc], op=ALU.add)
+                    nc.gpsimd.tensor_tensor(out=dst, in0=dst, in1=guard[:, hc], op=ALU.subtract)
+
+        def add_j(i):
+            g, t = divmod(i, 4)
+            for h in range(2):
+                hc = slice(512 * h, 512 * h + 512)
+                nc.vector.scalar_tensor_tensor(out=big[g][:, t, hc], in0=jps[i, h][:], scalar=0.5, in1=big[g][:, t, hc],
+                                               op0=ALU.mult, op1=ALU.add)
+
+        def row_exp(i):
+            g, t = divmod(i, 4)
+            nc.vector.tensor_reduce(out=rmax[:, i : i + 1], in_=big[g][:, t, :], axis=AX.X, op=ALU.max)
+            nc.vector.tensor_scalar(out=nrmax[:, i : i + 1], in0=rmax[:, i : i + 1], scalar1=-1.0, scalar2=LIFT, op0=ALU.mult, op1=ALU.add)
+            nc.scalar.activation(out=big[g][:, t, :], in_=big[g][:, t, :], func=ACT.Exp, bias=nrmax[:, i : i + 1], scale=1.0,
+                                 accum_out=rs2[:, i : i + 1])
+
+        def weight(i):
+            nc.vector.reciprocal(out=w1[:, i : i + 1], in_=rs2[:, i : i + 1])
+            nc.vector.tensor_scalar(out=w2[:, i : i + 1], in0=w1[:, i : i + 1], scalar1=W_SCALE, scalar2=None, op0=ALU.mult)
+
+        css = {}
+
+        def column_part(slots):
+            cs = psum.tile([P, 8], F32, name="jp" if slots[0] > 5 else "cs", bufs=2 if slots[0] > 5 else 1)
+            css[slots] = cs
+            for b in range(8):
+                for s in slots:
+                    nc.tensor.matmul(out=cs[:, b : b + 1], lhsT=big[s // 4][:, s % 4, P * b : P * b + P], rhs=w2[:, s : s + 1],
+                                     start=(s == slots[0]), stop=(s == slots[-1]))
+
+        def column_add(slots):
+            if slots[0] == 0:
+                nc.vector.tensor_copy(out=csum[:], in_=css[slots][:])
+            else:
+                nc.vector.tensor_tensor(out=csum[:], in0=css[slots][:], in1=csum[:], op=ALU.add)
+
+        x_g = scratch("x_int", [P, N, 4])
+        for pr in range(4):
+            turn_in(x_rows, pr, 0, x_g, X_ENG[pr])
+        y_g = scratch("y_int", [P, N, 4])
+        for pr in range(4):
+            turn_in(y_rows, pr, 0, y_g, Y_ENG[pr])
+
+        first_product(0)
+        c2_g = [scratch("c2_int", [P, N, 4]) for k in range(2)]
+        for n in range(8):
+            turn_in(c2_rows, n % 4, n // 4, c2_g[n // 4], C2_ENG[n])
+        nc.vector.tensor_tensor(out=dd[:, 0:4, :], in0=dd[:, 0:4, :], in1=dd[:, 4:8, :], op=ALU.max)
+        quantize_cv(0)
+        nc.vector.tensor_tensor(out=dd[:, 0:2, :], in0=dd[:, 0:2, :], in1=dd[:, 2:4, :], op=ALU.max)
+        nc.vector.tensor_tensor(out=dd[:, 0, :], in0=dd[:, 0, :], in1=dd[:, 1, :], op=ALU.max)
+        dT = psum.tile([P, 8, P], BF16, name="tp", bufs=3)
+        for b in range(8):
+            nc.tensor.transpose(dT[:, b, :], dd[:, 0, P * b : P * b + P], ident_b[:])
+        quantize(x_codes[:, 0, :], x_scales[:, 0, :], x_g[:].rearrange("p r j -> p (r j)"))
+        hT = keep.tile([P, 8], F32, name="hT")
+        hG = keep.tile([P, 8], F32, name="hG")
+        nc.vector.tensor_reduce(out=hT[:], in_=dT[:], axis=AX.X, op=ALU.max)
+        nc.vector.tensor_scalar(out=hG[:], in0=hT[:], scalar1=DEEP, scalar2=0.0, op0=ALU.add, op1=ALU.min)
+        guard = keep.tile([P, N], F32, name="guard")
+
+        def spread(col, half, unit):
+            bank = psum.tile([P, 4, P], F32, name="tp", bufs=3)
+            for b in range(4):
+                nc.tensor.matmul(out=bank[:, b, :], lhsT=col[:, 4 * half + b : 4 * half + b + 1].to_broadcast([P, P]),
+                                 rhs=unit[:], start=True, stop=True)
+            return bank
+
+        quantize(y_codes[:, 0, :], y_scales[:, 0, :], y_g[:].rearrange("p r j -> p (r j)"))
+        for h in range(2):
+            bank = spread(hG, h, ident)
+            nc.scalar.copy(out=guard[:, 512 * h : 512 * h + 512], in_=bank[:].rearrange("p b r -> p (b r)"))
+        for k in range(2):
+            quantize(c2_codes[:, k, :], c2_scales[:, k, :], c2_g[k][:].rearrange("p r j -> p (r j)"))
+        features(0)
+        first_product(1)
+        features(1)
+        for i in range(8):
+            if i < 6:
+                first_product(i + 2)
+            second_product(i)
+            if i < 6:
+                features(i + 2)
+            if i < 7:
+                quantize_cv(i + 1)
+            if i in (3, 5, 7):
+                column_part((i - 3, i - 2))
+            add_j(i)
+            if i > 0:
+                weight(i - 1)
+            row_exp(i)
+            if i in (3, 5, 7):
+                column_add((i - 3, i - 2))
+        column_part((6,))
+        weight(7)
+        column_part((7,))
+        column_add((6,))
+        column_add((7,))
+
+        rc1 = keep.tile([P, 8], F32, name="rc1")
+        nc.vector.reciprocal(out=rc1[:], in_=csum[:])
+        RC = [spread(rc1, h, ident_n) for h in range(2)]
+        o_codes = keep.tile([P, 2, N], U32, name="o_codes", align_bytes=64)
+        o_scales = keep.tile([P, 2, N], U8, name="o_scales", align_bytes=64)
+        o_int = {}
+
+        def scale_out(g, h):
+            hc = slice(512 * h, 512 * h + 512)
+            for t in range(4):
+                i = 4 * g + t
+                nc.vector.scalar_tensor_tensor(out=big[g][:, t, hc], in0=big[g][:, t, hc], scalar=w2[:, i : i + 1],
+                                               in1=RC[h][:].rearrange("p b r -> p (b r)"), op0=ALU.mult, op1=ALU.mult)
+            nc.sync.dma_start(out=out_0[512 * g : 512 * g + 512, hc].rearrange("(p t) m -> p t m", t=4), in_=big[g][:, :, hc])
+            o_int[g, h] = scratch("o_int", [P, 512, 4])
+
+        def interleave_out(g, h, split):
+            for a, b, eng in split:
+                src = big[g][:, :, 512 * h + a : 512 * h + b].rearrange("p t m -> p m t")
+                if eng == "s":
+                    nc.scalar.copy(out=o_int[g, h][:, a:b, :], in_=src)
+                else:
+                    nc.vector.tensor_copy(out=o_int[g, h][:, a:b, :], in_=src)
+
+        def quantize_out(g, h):
+            hc = slice(512 * h, 512 * h + 512)
+            quantize(o_codes[:, g, hc], o_scales[:, g, hc], o_int[g, h][:].rearrange("p m t -> p (m t)"))
+            nc.sync.dma_start(out=out_1[g, :, hc, :].rearrange("p m t -> p (m t)").bitcast(I32), in_=o_codes[:, g, hc].bitcast(I32))
+
+        scale_out(0, 0)
+        interleave_out(0, 0, ((0, 512, "s"),))
+        scale_out(0, 1)
+        interleave_out(0, 1, ((0, 512, "s"),))
+        quantize_out(0, 0)
+        scale_out(1, 0)
+        interleave_out(1, 0, ((0, 256, "s"), (256, 512, "v")))
+        quantize_out(0, 1)
+        scale_out(1, 1)
+        quantize_out(1, 0)
+        interleave_out(1, 1, ((0, 192, "s"), (192, 512, "v")))
+        quantize_out(1, 1)
+        for Q in range(4):
+            nc.sync.dma_start(out=out_2[:, 4 * Q : 4 * Q + 4, :].rearrange("g r m -> r g m").bitcast(I32),
+                              in_=o_scales[32 * Q : 32 * Q + 4, :, :].bitcast(I32))

@@ -25,11 +25,17 @@ W_SCALE = 2.0 ** 60
 C1_ENG = "ssssssss"
 X_ENG = "ssss"
 Y_ENG = "ssss"
-C2_ENG = "ssssssss"
-DD_EARLY = (0, 1, 2, 3)
-PLAN = "XXXXXXXX"
-CV_PLAN = "vggggggg"
-D_ENG = "v"
+C2_ENG = "svsvsvsv"
+FEAT_ENG = "ssssssssssssssss"
+A_ENG = "ssssssss"
+
+
+def weave(*streams):
+    longest = max(len(s) for s in streams)
+    for n in range(longest):
+        for s in streams:
+            if n < len(s):
+                s[n]()
 
 
 def tile_bilinearcouplingupdatesinkhorn_kernel(tc, lt, c1, c2, u, v, x, y, out_0, out_1, out_2):
@@ -40,44 +46,54 @@ def tile_bilinearcouplingupdatesinkhorn_kernel(tc, lt, c1, c2, u, v, x, y, out_0
         psum = ctx.enter_context(tc.psum_pool(name="psum", bufs=1))
         ctx.enter_context(tc.manual_schedule())
 
-        lt_sb = [keep.tile([P, 4, N], BF16, name="lt%d" % g, align_bytes=64) for g in range(2)]
-        c1_sb = [keep.tile([P, 4, N], BF16, name="c1_%d" % g, align_bytes=64) for g in range(2)]
-        x_sb = keep.tile([P, 2, 4, D], BF16, name="x_sb", align_bytes=64)
-        y_sb = keep.tile([P, 8, D], BF16, name="y_sb", align_bytes=64)
+        lt_sb = keep.tile([P, 8, N], BF16, name="lt_sb", align_bytes=64)
+        c1_sb = keep.tile([P, 8, N], BF16, name="c1_sb", tag="space0", align_bytes=64)
+        xy_sb = keep.tile([P, 2, 8, D], BF16, name="xy_sb", tag="space1", align_bytes=64)
         c2_sb = keep.tile([P, 8, N], BF16, name="c2_sb", align_bytes=64)
         u_raw = keep.tile([P, 2, 4], BF16, name="u_raw")
         v_raw = keep.tile([P, 2, 4], BF16, name="v_raw")
-        for g in range(2):
+        for q in range(4):
+            g, tp = divmod(q, 2)
             rows = lt[512 * g : 512 * g + 512, :].rearrange("(p t) m -> p t m", t=4)
-            for tp in range(2):
-                nc.sync.dma_start(out=lt_sb[g][:, 2 * tp : 2 * tp + 2, :], in_=rows[:, 2 * tp : 2 * tp + 2, :])
+            nc.sync.dma_start(out=lt_sb[:, 2 * q : 2 * q + 2, :], in_=rows[:, 2 * tp : 2 * tp + 2, :])
         nc.scalar.dma_start(out=u_raw[:], in_=u.rearrange("(g p t) -> p g t", p=P, t=4))
         nc.scalar.dma_start(out=v_raw[:], in_=v.rearrange("(g p t) -> p g t", p=P, t=4))
         for g in range(2):
-            nc.sync.dma_start(out=c1_sb[g][:], in_=c1[512 * g : 512 * g + 512, :].rearrange("(p t) m -> p t m", t=4))
-        nc.sync.dma_start(out=x_sb[:], in_=x.rearrange("(g p t) k -> p g t k", p=P, t=4))
-        nc.sync.dma_start(out=y_sb[:], in_=y.rearrange("(b p) k -> p b k", p=P))
+            nc.sync.dma_start(out=c1_sb[:, 4 * g : 4 * g + 4, :], in_=c1[512 * g : 512 * g + 512, :].rearrange("(p t) m -> p t m", t=4))
+        for g in range(2):
+            nc.sync.dma_start(out=xy_sb[:, 0, 4 * g : 4 * g + 4, :], in_=x[512 * g : 512 * g + 512, :].rearrange("(p t) k -> p t k", t=4))
+        nc.sync.dma_start(out=xy_sb[:, 1, :, :], in_=y.rearrange("(b p) k -> p b k", p=P))
         for q in range(2):
             nc.sync.dma_start(out=c2_sb[:, 4 * q : 4 * q + 4, :], in_=c2[512 * q : 512 * q + 512, :].rearrange("(b p) k -> p b k", p=P))
 
         ident = keep.tile([P, P], F32, name="ident")
         make_identity(nc, ident[:])
-        ident_n = keep.tile([P, P], F32, name="ident_n")
-        nc.gpsimd.tensor_scalar(out=ident_n[:], in0=ident[:], scalar1=float(N), scalar2=0.0, op0=ALU.mult, op1=ALU.add)
         ident_b = keep.tile([P, P], BF16, name="ident_b")
         make_identity(nc, ident_b[:])
 
+        def col(name):
+            return keep.tile([P, 8], F32, name=name)
+
         u_f = keep.tile([P, 2, 4], F32, name="u_f")
         v_f = keep.tile([P, 2, 4], F32, name="v_f")
-        mx = keep.tile([P, 8], F32, name="mx")
-        nmx = keep.tile([P, 8], F32, name="nmx")
-        rs = keep.tile([P, 8], F32, name="rs")
-        rrs = keep.tile([P, 8], F32, name="rrs")
-        amp = keep.tile([P, 8], F32, name="amp")
+        mx, nmx, rs, rrs, amp = col("mx"), col("nmx"), col("rs"), col("rrs"), col("amp")
+        hT, hG, lift_t = col("hT"), col("hG"), col("lift_t")
+        rmax, nrmax, rs2, w1, w2, csum, rc1 = col("rmax"), col("nrmax"), col("rs2"), col("w1"), col("w2"), col("csum"), col("rc1")
         dd = keep.tile([P, 8, N], BF16, name="dd")
         big = [keep.tile([P, 4, N], F32, name="big%d" % g) for g in range(2)]
-        t_codes = keep.tile([P, 2, N], U32, name="t_codes", align_bytes=64)
-        t_scales = keep.tile([P, 2, N], U8, name="t_scales", align_bytes=64)
+
+        def planes(name, kappas):
+            codes = keep.tile([P, kappas, N], U32, name=name + "_codes", align_bytes=64)
+            scales = keep.tile([P, kappas, N], U8, name=name + "_scales", align_bytes=64)
+            return codes, scales
+
+        t_codes, t_scales = planes("t", 2)
+        c1_codes, c1_scales = planes("c1", 2)
+        x_codes, x_scales = planes("x", 1)
+        y_codes, y_scales = planes("y", 1)
+        c2_codes, c2_scales = planes("c2", 2)
+        o_codes, o_scales = planes("o", 2)
+        feat_scale = 0.5 / (float(D) ** 0.5)
 
         def scratch(name, shape):
             return rot.tile(shape, BF16, name=name, tag="grouped", align_bytes=64, bufs=5)
@@ -85,48 +101,64 @@ def tile_bilinearcouplingupdatesinkhorn_kernel(tc, lt, c1, c2, u, v, x, y, out_0
         def quantize(codes, scales, grouped):
             nc.vector.quantize_mx(out=codes.bitcast(FP8X4), scales=scales, in_=grouped)
 
-        def tree(qs):
-            level = {}
-            for q in qs:
-                g, tp = divmod(q, 2)
-                level[q] = lt_sb[g][:, 2 * tp : 2 * tp + 2, :]
-            width, lvl = N, 0
-            while width > 32:
-                half = width // 2
-                for q in qs:
-                    m = rot.tile([P, 2, half], BF16, name="m%d" % lvl, bufs=3)
-                    nc.vector.tensor_tensor(out=m[:], in0=level[q][:, :, 0:half], in1=level[q][:, :, half:width], op=ALU.max)
-                    level[q] = m[:]
-                width, lvl = half, lvl + 1
-            for q in qs:
-                nc.vector.tensor_reduce(out=mx[:, 2 * q : 2 * q + 2], in_=level[q], axis=AX.X, op=ALU.max)
-            s = slice(2 * qs[0], 2 * qs[-1] + 2)
-            nc.vector.tensor_scalar(out=nmx[:, s], in0=mx[:, s], scalar1=-1.0, scalar2=None, op0=ALU.mult)
+        def quantize_k(codes, scales, k, grouped):
+            quantize(codes[:, k, :], scales[:, k, :], grouped[:].rearrange("p r j -> p (r j)"))
+
+        def tree(q):
+            state = {"src": lt_sb[:, 2 * q : 2 * q + 2, :]}
+
+            def level(lvl):
+                half = 512 >> lvl
+                m = rot.tile([P, 2, half], BF16, name="m%d" % lvl)
+                src = state["src"]
+                nc.vector.tensor_tensor(out=m[:], in0=src[:, :, 0:half], in1=src[:, :, half : 2 * half], op=ALU.max)
+                state["src"] = m[:]
+
+            def last():
+                nc.vector.tensor_reduce(out=mx[:, 2 * q : 2 * q + 2], in_=state["src"], axis=AX.X, op=ALU.max)
+
+            def negative():
+                nc.vector.tensor_scalar(out=nmx[:, 2 * q : 2 * q + 2], in0=mx[:, 2 * q : 2 * q + 2], scalar1=-1.0, scalar2=None, op0=ALU.mult)
+
+            return [lambda lvl=lvl: level(lvl) for lvl in range(5)] + [last, negative]
 
         def exps(q):
             for s in (2 * q, 2 * q + 1):
                 g, t = divmod(s, 4)
-                nc.scalar.activation(out=big[g][:, t, :], in_=lt_sb[g][:, t, :], func=ACT.Exp, bias=nmx[:, s : s + 1],
+                nc.scalar.activation(out=big[g][:, t, :], in_=lt_sb[:, s, :], func=ACT.Exp, bias=nmx[:, s : s + 1],
                                      scale=1.0, accum_out=rs[:, s : s + 1])
 
         def depth(q):
-            for s in (2 * q, 2 * q + 1):
-                g, t = divmod(s, 4)
-                eng = nc.gpsimd if D_ENG == "g" else nc.vector
-                eng.tensor_scalar(out=dd[:, s, :], in0=lt_sb[g][:, t, :], scalar1=nmx[:, s : s + 1],
-                                  scalar2=1.0, op0=ALU.add, op1=ALU.mult)
+            def one(s):
+                nc.vector.tensor_scalar(out=dd[:, s, :], in0=lt_sb[:, s, :], scalar1=nmx[:, s : s + 1], scalar2=None, op0=ALU.add)
+
+            return [lambda s=s: one(s) for s in (2 * q, 2 * q + 1)]
+
+        def guard_tree():
+            def level(width):
+                if width:
+                    nc.vector.tensor_tensor(out=dd[:, 0:width, :], in0=dd[:, 0:width, :], in1=dd[:, width : 2 * width, :], op=ALU.max)
+
+            return [lambda width=width: level(width) for width in (4, 2, 1)]
 
         tb = [scratch("tb%d" % g, [P, 4, N]) for g in range(2)]
 
         def deviation(q):
             g, tp = divmod(q, 2)
             s = slice(2 * q, 2 * q + 2)
-            nc.vector.reciprocal(out=rrs[:, s], in_=rs[:, s])
-            nc.vector.scalar_tensor_tensor(out=amp[:, s], in0=rrs[:, s], scalar=float(N),
-                                           in1=u_f[:, g, 2 * tp : 2 * tp + 2], op0=ALU.mult, op1=ALU.mult)
-            for t in (2 * tp, 2 * tp + 1):
+
+            def inverse():
+                nc.vector.reciprocal(out=rrs[:, s], in_=rs[:, s])
+
+            def gain():
+                nc.vector.scalar_tensor_tensor(out=amp[:, s], in0=rrs[:, s], scalar=float(N),
+                                               in1=u_f[:, g, 2 * tp : 2 * tp + 2], op0=ALU.mult, op1=ALU.mult)
+
+            def apply(t):
                 nc.vector.tensor_scalar(out=tb[g][:, t, :], in0=big[g][:, t, :], scalar1=amp[:, 4 * g + t : 4 * g + t + 1],
                                         scalar2=u_f[:, g, t : t + 1], op0=ALU.mult, op1=ALU.subtract)
+
+            return [inverse, gain] + [lambda t=t: apply(t) for t in (2 * tp, 2 * tp + 1)]
 
         t_int = {}
 
@@ -140,14 +172,11 @@ def tile_bilinearcouplingupdatesinkhorn_kernel(tc, lt, c1, c2, u, v, x, y, out_0
             else:
                 nc.scalar.copy(out=o, in_=i)
 
-        def quantize_t(g):
-            quantize(t_codes[:, g, :], t_scales[:, g, :], t_int[g][:].rearrange("p r j -> p (r j)"))
-
         def turn_in(rows, pr, kappa, dst, eng):
             dst_w = dst[:].rearrange("p r j -> p (r j)").bitcast(F32).rearrange("p (s r w) -> p s r w", s=8, w=2)
-            bank = psum.tile([P, 2, 2, P], F32, name="tp", bufs=3)
+            bank = psum.tile([P, 2, 2, P], F32, name="tp", bufs=4)
             for s in range(2):
-                words = rows(2 * pr + s).bitcast(F32)
+                words = rows[:, 2 * pr + s, :].bitcast(F32)
                 for w in range(2):
                     nc.tensor.transpose(bank[:, s, w, :], words[:, 256 * kappa + w : 256 * kappa + 256 : 2], ident[:])
             o = dst_w[:, 2 * pr : 2 * pr + 2, :, :]
@@ -157,94 +186,31 @@ def tile_bilinearcouplingupdatesinkhorn_kernel(tc, lt, c1, c2, u, v, x, y, out_0
             else:
                 nc.scalar.copy(out=o, in_=i)
 
-        def planes(name, kappas):
-            codes = keep.tile([P, kappas, N], U32, name=name + "_codes", align_bytes=64)
-            scales = keep.tile([P, kappas, N], U8, name=name + "_scales", align_bytes=64)
-            return codes, scales
-
-        def c1_rows(s):
-            return c1_sb[s // 4][:, s % 4, :]
-
-        def x_rows(s):
-            return x_sb[:, s // 4, s % 4, :]
-
-        def y_rows(s):
-            return y_sb[:, s, :]
-
-        def c2_rows(s):
-            return c2_sb[:, s, :]
-
-        c1_codes, c1_scales = planes("c1", 2)
-        x_codes, x_scales = planes("x", 1)
-        y_codes, y_scales = planes("y", 1)
-        c2_codes, c2_scales = planes("c2", 2)
-        feat_scale = 0.5 / (float(D) ** 0.5)
-
-        tree((0,))
-        exps(0)
-        tree((1,))
-        exps(1)
-        nc.vector.tensor_copy(out=u_f[:], in_=u_raw[:])
-        nc.vector.tensor_copy(out=v_f[:], in_=v_raw[:])
-        tree((2, 3))
-        exps(2)
-        exps(3)
-        deviation(0)
-        deviation(1)
-        c1_g = [scratch("c1_int", [P, N, 4]) for k in range(2)]
-
-        def turn_c1(half):
-            for k in range(2):
-                for pr in (2 * half, 2 * half + 1):
-                    turn_in(c1_rows, pr, k, c1_g[k], C1_ENG[4 * half + 2 * k + pr % 2])
-
-        turn_c1(0)
-        interleave_t(0, 0, "v")
-        interleave_t(0, 1, "s")
-        deviation(2)
-        deviation(3)
-        turn_c1(1)
-        interleave_t(1, 0, "v")
-        interleave_t(1, 1, "s")
-        for q in DD_EARLY:
-            depth(q)
-        quantize_t(0)
-        for k in range(2):
-            quantize(c1_codes[:, k, :], c1_scales[:, k, :], c1_g[k][:].rearrange("p r j -> p (r j)"))
-        quantize_t(1)
-
-        rmax = keep.tile([P, 8], F32, name="rmax")
-        nrmax = keep.tile([P, 8], F32, name="nrmax")
-        rs2 = keep.tile([P, 8], F32, name="rs2")
-        w1 = keep.tile([P, 8], F32, name="w1")
-        w2 = keep.tile([P, 8], F32, name="w2")
-        csum = keep.tile([P, 8], F32, name="csum")
         cv = {}
         jps = {}
+        feat_t = {}
+        ct = {}
 
         def first_product(i):
             cols = slice(P * i, P * i + P)
-            cv_int = rot.tile([P, 2, P, 4], BF16, name="cv_int", align_bytes=64, bufs=3)
-            cv_codes = rot.tile([P, 2, P], U32, name="cv_codes", align_bytes=64, bufs=3)
-            cv_scales = rot.tile([P, 2, P], U8, name="cv_scales", align_bytes=64, bufs=3)
-            cv[i] = (cv_int, cv_codes, cv_scales)
             for G in range(2):
                 ctp = psum.tile([P, 4, P], F32, name="ctp", bufs=2)
+                ct[i, G] = ctp
                 for T in range(4):
                     mcols = slice(512 * G + P * T, 512 * G + P * T + P)
                     for k in range(2):
                         nc.tensor.matmul_mx(out=ctp[:, T, :], lhsT=t_codes[:, k, mcols].bitcast(FP8X4), lhsT_scale=t_scales[:, k, mcols],
                                             rhs=c1_codes[:, k, cols].bitcast(FP8X4), rhs_scale=c1_scales[:, k, cols],
                                             start=(k == 0), stop=(k == 1))
-                if CV_PLAN[i] == "v":
-                    nc.vector.tensor_tensor(out=cv_int[:, G, :, :], in0=ctp[:].rearrange("p T i -> p i T"),
-                                            in1=v_f[:, G : G + 1, :].to_broadcast([P, P, 4]), op=ALU.mult)
-                else:
-                    flat = rot.tile([P, 4, P], BF16, name="cv_flat", bufs=4)
-                    for T in range(4):
-                        nc.scalar.activation(out=flat[:, T, :], in_=ctp[:, T, :], func=ACT.Copy, scale=v_f[:, G, T : T + 1])
-                    nc.gpsimd.tensor_scalar(out=cv_int[:, G, :, :], in0=flat[:].rearrange("p T i -> p i T"), scalar1=1.0, scalar2=0.0,
-                                            op0=ALU.mult, op1=ALU.add)
+
+        def gain_cv(i, G):
+            if G == 0:
+                cv_int = rot.tile([P, 2, P, 4], BF16, name="cv_int", align_bytes=64, bufs=3)
+                cv_codes = rot.tile([P, 2, P], U32, name="cv_codes", align_bytes=64, bufs=3)
+                cv_scales = rot.tile([P, 2, P], U8, name="cv_scales", align_bytes=64, bufs=3)
+                cv[i] = (cv_int, cv_codes, cv_scales)
+            nc.vector.tensor_tensor(out=cv[i][0][:, G, :, :], in0=ct[i, G][:].rearrange("p T i -> p i T"),
+                                    in1=v_f[:, G : G + 1, :].to_broadcast([P, P, 4]), op=ALU.mult)
 
         def quantize_cv(i):
             cv_int, cv_codes, cv_scales = cv[i]
@@ -262,50 +228,70 @@ def tile_bilinearcouplingupdatesinkhorn_kernel(tc, lt, c1, c2, u, v, x, y, out_0
                                         rhs=c2_codes[:, k, hc].bitcast(FP8X4), rhs_scale=c2_scales[:, k, hc],
                                         start=(k == 0), stop=(k == 1))
 
-        def features(i):
-            g, t = divmod(i, 4)
-            cols = slice(P * i, P * i + P)
-            for h in range(2):
-                hc = slice(512 * h, 512 * h + 512)
-                dst = big[g][:, t, hc]
-                ft = psum.tile([P, 512], F32, name="tp", bufs=3)
-                nc.tensor.matmul_mx(out=ft[:], lhsT=x_codes[:, 0, cols].bitcast(FP8X4), lhsT_scale=x_scales[:, 0, cols],
-                                    rhs=y_codes[:, 0, hc].bitcast(FP8X4), rhs_scale=y_scales[:, 0, hc], start=True, stop=True)
-                if PLAN[i] == "Z":
-                    nc.vector.scalar_tensor_tensor(out=dst, in0=ft[:], scalar=feat_scale, in1=lt_sb[g][:, t, hc],
-                                                   op0=ALU.mult, op1=ALU.add)
-                    nc.gpsimd.tensor_tensor(out=dst, in0=dst, in1=guard[:, hc], op=ALU.subtract)
-                elif PLAN[i] == "X":
-                    nc.vector.scalar_tensor_tensor(out=dst, in0=ft[:], scalar=feat_scale, in1=guard[:, hc],
-                                                   op0=ALU.mult, op1=ALU.subtract)
-                    nc.gpsimd.tensor_tensor(out=dst, in0=dst, in1=lt_sb[g][:, t, hc], op=ALU.add)
-                else:
-                    nc.scalar.activation(out=dst, in_=ft[:], func=ACT.Copy, scale=feat_scale)
-                    nc.gpsimd.tensor_tensor(out=dst, in0=dst, in1=lt_sb[g][:, t, hc], op=ALU.add)
-                    nc.gpsimd.tensor_tensor(out=dst, in0=dst, in1=guard[:, hc], op=ALU.subtract)
+        def features(g, b):
+            ft = psum.tile([P, 512], F32, name="tp", bufs=4)
+            hc = slice(512 * g, 512 * g + 512)
+            lcols = slice(P * b, P * b + P)
+            nc.tensor.matmul_mx(out=ft[:], lhsT=y_codes[:, 0, lcols].bitcast(FP8X4), lhsT_scale=y_scales[:, 0, lcols],
+                                rhs=x_codes[:, 0, hc].bitcast(FP8X4), rhs_scale=x_scales[:, 0, hc], start=True, stop=True)
+            if g not in feat_t:
+                feat_t[g] = keep.tile([P, 8, 512], F32, name="feat_t", tag="space%d" % g, align_bytes=64)
+            dst = feat_t[g][:, b, :]
+            if FEAT_ENG[8 * g + b] == "v":
+                nc.vector.tensor_scalar(out=dst, in0=ft[:], scalar1=feat_scale, scalar2=lift_t[:, b : b + 1],
+                                        op0=ALU.mult, op1=ALU.add)
+            else:
+                nc.scalar.activation(out=dst, in_=ft[:], func=ACT.Identity, scale=feat_scale, bias=lift_t[:, b : b + 1])
 
-        def add_j(i):
+        def make_a(i):
             g, t = divmod(i, 4)
+            banks = [psum.tile([P, 4, P], F32, name="tp", bufs=4) for h in range(2)]
             for h in range(2):
-                hc = slice(512 * h, 512 * h + 512)
-                nc.vector.scalar_tensor_tensor(out=big[g][:, t, hc], in0=jps[i, h][:], scalar=0.5, in1=big[g][:, t, hc],
-                                               op0=ALU.mult, op1=ALU.add)
+                nc.tensor.matmul(out=banks[h][:].rearrange("p b r -> p (b r)"), lhsT=ident_b[:], rhs=lt_sb[:, i, 512 * h : 512 * h + 512],
+                                 start=True, stop=False)
+            for h in range(2):
+                for b in range(4):
+                    nc.tensor.matmul(out=banks[h][:, b, :], lhsT=feat_t[g][:, 4 * h + b, P * t : P * t + P], rhs=ident[:],
+                                     start=False, stop=(b == 3), is_transpose=True)
+            for h in range(2):
+                dst = big[g][:, t, 512 * h : 512 * h + 512]
+                src = banks[h][:].rearrange("p b r -> p (b r)")
+                if A_ENG[i] == "v":
+                    nc.vector.tensor_copy(out=dst, in_=src)
+                else:
+                    nc.scalar.copy(out=dst, in_=src)
+
+        def add_j(i, h):
+            g, t = divmod(i, 4)
+            hc = slice(512 * h, 512 * h + 512)
+            nc.vector.scalar_tensor_tensor(out=big[g][:, t, hc], in0=jps[i, h][:], scalar=0.5, in1=big[g][:, t, hc],
+                                           op0=ALU.mult, op1=ALU.add)
+
+        def row_max(i):
+            g, t = divmod(i, 4)
+            nc.vector.tensor_reduce(out=rmax[:, i : i + 1], in_=big[g][:, t, :], axis=AX.X, op=ALU.max)
+
+        def row_shift(i):
+            nc.vector.tensor_scalar(out=nrmax[:, i : i + 1], in0=rmax[:, i : i + 1], scalar1=-1.0, scalar2=LIFT, op0=ALU.mult, op1=ALU.add)
 
         def row_exp(i):
             g, t = divmod(i, 4)
-            nc.vector.tensor_reduce(out=rmax[:, i : i + 1], in_=big[g][:, t, :], axis=AX.X, op=ALU.max)
-            nc.vector.tensor_scalar(out=nrmax[:, i : i + 1], in0=rmax[:, i : i + 1], scalar1=-1.0, scalar2=LIFT, op0=ALU.mult, op1=ALU.add)
             nc.scalar.activation(out=big[g][:, t, :], in_=big[g][:, t, :], func=ACT.Exp, bias=nrmax[:, i : i + 1], scale=1.0,
                                  accum_out=rs2[:, i : i + 1])
 
         def weight(i):
-            nc.vector.reciprocal(out=w1[:, i : i + 1], in_=rs2[:, i : i + 1])
-            nc.vector.tensor_scalar(out=w2[:, i : i + 1], in0=w1[:, i : i + 1], scalar1=W_SCALE, scalar2=None, op0=ALU.mult)
+            def inverse():
+                nc.vector.reciprocal(out=w1[:, i : i + 1], in_=rs2[:, i : i + 1])
+
+            def scaled():
+                nc.vector.tensor_scalar(out=w2[:, i : i + 1], in0=w1[:, i : i + 1], scalar1=W_SCALE, scalar2=None, op0=ALU.mult)
+
+            return [inverse, scaled]
 
         css = {}
 
         def column_part(slots):
-            cs = psum.tile([P, 8], F32, name="jp" if slots[0] > 5 else "cs", bufs=2 if slots[0] > 5 else 1)
+            cs = psum.tile([P, 8], F32, name="tp", bufs=4)
             css[slots] = cs
             for b in range(8):
                 for s in slots:
@@ -314,78 +300,142 @@ def tile_bilinearcouplingupdatesinkhorn_kernel(tc, lt, c1, c2, u, v, x, y, out_0
 
         def column_add(slots):
             if slots[0] == 0:
-                nc.vector.tensor_copy(out=csum[:], in_=css[slots][:])
+                nc.vector.tensor_scalar(out=csum[:], in0=css[slots][:], scalar1=1.0 / N, scalar2=None, op0=ALU.mult)
             else:
-                nc.vector.tensor_tensor(out=csum[:], in0=css[slots][:], in1=csum[:], op=ALU.add)
+                nc.vector.scalar_tensor_tensor(out=csum[:], in0=css[slots][:], scalar=1.0 / N, in1=csum[:], op0=ALU.mult, op1=ALU.add)
 
-        x_g = scratch("x_int", [P, N, 4])
-        for pr in range(4):
-            turn_in(x_rows, pr, 0, x_g, X_ENG[pr])
-        y_g = scratch("y_int", [P, N, 4])
-        for pr in range(4):
-            turn_in(y_rows, pr, 0, y_g, Y_ENG[pr])
+        dT = {}
 
-        first_product(0)
-        c2_g = [scratch("c2_int", [P, N, 4]) for k in range(2)]
-        for n in range(8):
-            turn_in(c2_rows, n % 4, n // 4, c2_g[n // 4], C2_ENG[n])
-        nc.vector.tensor_tensor(out=dd[:, 0:4, :], in0=dd[:, 0:4, :], in1=dd[:, 4:8, :], op=ALU.max)
-        quantize_cv(0)
-        nc.vector.tensor_tensor(out=dd[:, 0:2, :], in0=dd[:, 0:2, :], in1=dd[:, 2:4, :], op=ALU.max)
-        nc.vector.tensor_tensor(out=dd[:, 0, :], in0=dd[:, 0, :], in1=dd[:, 1, :], op=ALU.max)
-        dT = psum.tile([P, 8, P], BF16, name="tp", bufs=3)
-        for b in range(8):
-            nc.tensor.transpose(dT[:, b, :], dd[:, 0, P * b : P * b + P], ident_b[:])
-        quantize(x_codes[:, 0, :], x_scales[:, 0, :], x_g[:].rearrange("p r j -> p (r j)"))
-        hT = keep.tile([P, 8], F32, name="hT")
-        hG = keep.tile([P, 8], F32, name="hG")
-        nc.vector.tensor_reduce(out=hT[:], in_=dT[:], axis=AX.X, op=ALU.max)
-        nc.vector.tensor_scalar(out=hG[:], in0=hT[:], scalar1=DEEP, scalar2=0.0, op0=ALU.add, op1=ALU.min)
-        guard = keep.tile([P, N], F32, name="guard")
+        def guard_turn():
+            dT[0] = psum.tile([P, 8, P], BF16, name="tp", bufs=4)
+            for b in range(8):
+                nc.tensor.transpose(dT[0][:, b, :], dd[:, 0, P * b : P * b + P], ident_b[:])
 
-        def spread(col, half, unit):
-            bank = psum.tile([P, 4, P], F32, name="tp", bufs=3)
+        def guard_end():
+            def deepest():
+                nc.vector.tensor_reduce(out=hT[:], in_=dT[0][:], axis=AX.X, op=ALU.max)
+
+            def cut():
+                nc.vector.tensor_scalar(out=hG[:], in0=hT[:], scalar1=DEEP, scalar2=0.0, op0=ALU.add, op1=ALU.min)
+
+            def sign():
+                nc.vector.tensor_scalar(out=lift_t[:], in0=hG[:], scalar1=-1.0, scalar2=None, op0=ALU.mult)
+
+            return [deepest, cut, sign]
+
+        def spread(c, half):
+            bank = psum.tile([P, 4, P], F32, name="tp", bufs=4)
             for b in range(4):
-                nc.tensor.matmul(out=bank[:, b, :], lhsT=col[:, 4 * half + b : 4 * half + b + 1].to_broadcast([P, P]),
-                                 rhs=unit[:], start=True, stop=True)
+                nc.tensor.transpose(bank[:, b, :], c[:, 4 * half + b : 4 * half + b + 1].to_broadcast([P, P]), ident[:])
             return bank
 
-        quantize(y_codes[:, 0, :], y_scales[:, 0, :], y_g[:].rearrange("p r j -> p (r j)"))
-        for h in range(2):
-            bank = spread(hG, h, ident)
-            nc.scalar.copy(out=guard[:, 512 * h : 512 * h + 512], in_=bank[:].rearrange("p b r -> p (b r)"))
-        for k in range(2):
-            quantize(c2_codes[:, k, :], c2_scales[:, k, :], c2_g[k][:].rearrange("p r j -> p (r j)"))
-        features(0)
+        def widen_u():
+            nc.vector.tensor_copy(out=u_f[:], in_=u_raw[:])
+
+        def widen_v():
+            nc.vector.tensor_copy(out=v_f[:], in_=v_raw[:])
+
+        weave(tree(0))
+        exps(0)
+        weave(tree(1), [widen_u, widen_v] + depth(0))
+        exps(1)
+        weave(tree(2), tree(3), depth(1))
+        exps(2)
+        exps(3)
+        c1_g = [scratch("c1_int", [P, N, 4]) for k in range(2)]
+
+        def turn_c1(half):
+            for k in range(2):
+                for pr in (2 * half, 2 * half + 1):
+                    turn_in(c1_sb, pr, k, c1_g[k], C1_ENG[4 * half + 2 * k + pr % 2])
+
+        weave(deviation(0), depth(2))
+        weave(deviation(1), depth(3))
+        turn_c1(0)
+        gt = guard_tree()
+        gt[0]()
+        interleave_t(0, 0, "v")
+        weave(deviation(2), gt[1:])
+        weave(deviation(3))
+        interleave_t(0, 1, "s")
+        interleave_t(1, 1, "s")
+        turn_c1(1)
+        guard_turn()
+        interleave_t(1, 0, "v")
+        quantize_k(t_codes, t_scales, 0, t_int[0])
+        ge = guard_end()
+        ge[0]()
+        quantize_k(t_codes, t_scales, 1, t_int[1])
+        ge[1]()
+        x_g = scratch("x_int", [P, N, 4])
+        y_g = scratch("y_int", [P, N, 4])
+        for pr in range(4):
+            turn_in(xy_sb[:, 0, :, :], pr, 0, x_g, X_ENG[pr])
+        for pr in range(4):
+            turn_in(xy_sb[:, 1, :, :], pr, 0, y_g, Y_ENG[pr])
+        quantize_k(c1_codes, c1_scales, 0, c1_g[0])
+        ge[2]()
+        quantize_k(c1_codes, c1_scales, 1, c1_g[1])
+        first_product(0)
+        quantize_k(x_codes, x_scales, 0, x_g)
+        gain_cv(0, 0)
+        gain_cv(0, 1)
+        quantize_k(y_codes, y_scales, 0, y_g)
+        c2_g = [scratch("c2_int", [P, N, 4]) for k in range(2)]
+        for n in range(4):
+            turn_in(c2_sb, n, 0, c2_g[0], C2_ENG[n])
+        quantize_cv(0)
         first_product(1)
-        features(1)
+        for b in range(4):
+            features(0, b)
+        gain_cv(1, 0)
+        gain_cv(1, 1)
+        quantize_k(c2_codes, c2_scales, 0, c2_g[0])
+        for n in range(4):
+            turn_in(c2_sb, n, 1, c2_g[1], C2_ENG[4 + n])
+        for b in range(4, 8):
+            features(0, b)
+        quantize_cv(1)
+        first_product(2)
+        make_a(0)
+        quantize_k(c2_codes, c2_scales, 1, c2_g[1])
+        make_a(1)
         for i in range(8):
-            if i < 6:
-                first_product(i + 2)
             second_product(i)
             if i < 6:
-                features(i + 2)
-            if i < 7:
-                quantize_cv(i + 1)
+                gain_cv(i + 2, 0)
+                gain_cv(i + 2, 1)
+            if i < 5:
+                first_product(i + 3)
+            if i < 2:
+                for b in range(4 * i, 4 * i + 4):
+                    features(1, b)
             if i in (3, 5, 7):
                 column_part((i - 3, i - 2))
-            add_j(i)
+            if i < 6:
+                make_a(i + 2)
+            add_j(i, 0)
+            add_j(i, 1)
+            if i < 6:
+                quantize_cv(i + 2)
+            row_max(i)
+            w = weight(i - 1) if i > 0 else [None, None]
             if i > 0:
-                weight(i - 1)
+                w[0]()
+            row_shift(i)
             row_exp(i)
+            if i > 0:
+                w[1]()
             if i in (3, 5, 7):
                 column_add((i - 3, i - 2))
         column_part((6,))
-        weight(7)
+        weave(weight(7))
         column_part((7,))
         column_add((6,))
         column_add((7,))
 
-        rc1 = keep.tile([P, 8], F32, name="rc1")
         nc.vector.reciprocal(out=rc1[:], in_=csum[:])
-        RC = [spread(rc1, h, ident_n) for h in range(2)]
-        o_codes = keep.tile([P, 2, N], U32, name="o_codes", align_bytes=64)
-        o_scales = keep.tile([P, 2, N], U8, name="o_scales", align_bytes=64)
+        RC = [spread(rc1, h) for h in range(2)]
         o_int = {}
 
         def scale_out(g, h):

from contextlib import ExitStack

import concourse.mybir as mybir
from concourse.masks import make_identity

F32 = mybir.dt.float32
BF16 = mybir.dt.bfloat16
U32 = mybir.dt.uint32
I32 = mybir.dt.int32
U8 = mybir.dt.uint8
FP8X4 = mybir.dt.float8_e4m3fn_x4
ACT = mybir.ActivationFunctionType
ALU = mybir.AluOpType
AX = mybir.AxisListType

P = 128
N = 1024
D = 512
FLOPS = 2 * N * N * N * 2 + 2 * N * N * D

LIFT = 72.0
DEEP = 90.0
W_SCALE = 2.0 ** 60

C1_ENG = "ssssssss"
X_ENG = "ssss"
Y_ENG = "ssss"
C2_ENG = "svsvsvsv"
FEAT_ENG = "ssssssssssssssss"
A_ENG = "ssssssss"


def weave(*streams):
    longest = max(len(s) for s in streams)
    for n in range(longest):
        for s in streams:
            if n < len(s):
                s[n]()


def tile_bilinearcouplingupdatesinkhorn_kernel(tc, lt, c1, c2, u, v, x, y, out_0, out_1, out_2):
    nc = tc.nc
    with ExitStack() as ctx:
        keep = ctx.enter_context(tc.tile_pool(name="keep", bufs=1))
        rot = ctx.enter_context(tc.tile_pool(name="rot", bufs=2))
        psum = ctx.enter_context(tc.psum_pool(name="psum", bufs=1))
        ctx.enter_context(tc.manual_schedule())

        lt_sb = keep.tile([P, 8, N], BF16, name="lt_sb", align_bytes=64)
        c1_sb = keep.tile([P, 8, N], BF16, name="c1_sb", tag="space0", align_bytes=64)
        xy_sb = keep.tile([P, 2, 8, D], BF16, name="xy_sb", tag="space1", align_bytes=64)
        c2_sb = keep.tile([P, 8, N], BF16, name="c2_sb", align_bytes=64)
        u_raw = keep.tile([P, 2, 4], BF16, name="u_raw")
        v_raw = keep.tile([P, 2, 4], BF16, name="v_raw")
        for q in range(4):
            g, tp = divmod(q, 2)
            rows = lt[512 * g : 512 * g + 512, :].rearrange("(p t) m -> p t m", t=4)
            nc.sync.dma_start(out=lt_sb[:, 2 * q : 2 * q + 2, :], in_=rows[:, 2 * tp : 2 * tp + 2, :])
        nc.scalar.dma_start(out=u_raw[:], in_=u.rearrange("(g p t) -> p g t", p=P, t=4))
        nc.scalar.dma_start(out=v_raw[:], in_=v.rearrange("(g p t) -> p g t", p=P, t=4))
        for g in range(2):
            nc.sync.dma_start(out=c1_sb[:, 4 * g : 4 * g + 4, :], in_=c1[512 * g : 512 * g + 512, :].rearrange("(p t) m -> p t m", t=4))
        for g in range(2):
            nc.sync.dma_start(out=xy_sb[:, 0, 4 * g : 4 * g + 4, :], in_=x[512 * g : 512 * g + 512, :].rearrange("(p t) k -> p t k", t=4))
        nc.sync.dma_start(out=xy_sb[:, 1, :, :], in_=y.rearrange("(b p) k -> p b k", p=P))
        for q in range(2):
            nc.sync.dma_start(out=c2_sb[:, 4 * q : 4 * q + 4, :], in_=c2[512 * q : 512 * q + 512, :].rearrange("(b p) k -> p b k", p=P))

        ident = keep.tile([P, P], F32, name="ident")
        make_identity(nc, ident[:])
        ident_b = keep.tile([P, P], BF16, name="ident_b")
        make_identity(nc, ident_b[:])

        def col(name):
            return keep.tile([P, 8], F32, name=name)

        u_f = keep.tile([P, 2, 4], F32, name="u_f")
        v_f = keep.tile([P, 2, 4], F32, name="v_f")
        mx, nmx, rs, rrs, amp = col("mx"), col("nmx"), col("rs"), col("rrs"), col("amp")
        hT, hG, lift_t = col("hT"), col("hG"), col("lift_t")
        rmax, nrmax, rs2, w1, w2, csum, rc1 = col("rmax"), col("nrmax"), col("rs2"), col("w1"), col("w2"), col("csum"), col("rc1")
        dd = keep.tile([P, 8, N], BF16, name="dd")
        big = [keep.tile([P, 4, N], F32, name="big%d" % g) for g in range(2)]

        def planes(name, kappas):
            codes = keep.tile([P, kappas, N], U32, name=name + "_codes", align_bytes=64)
            scales = keep.tile([P, kappas, N], U8, name=name + "_scales", align_bytes=64)
            return codes, scales

        t_codes, t_scales = planes("t", 2)
        c1_codes, c1_scales = planes("c1", 2)
        x_codes, x_scales = planes("x", 1)
        y_codes, y_scales = planes("y", 1)
        c2_codes, c2_scales = planes("c2", 2)
        o_codes, o_scales = planes("o", 2)
        feat_scale = 0.5 / (float(D) ** 0.5)

        def scratch(name, shape):
            return rot.tile(shape, BF16, name=name, tag="grouped", align_bytes=64, bufs=5)

        def quantize(codes, scales, grouped):
            nc.vector.quantize_mx(out=codes.bitcast(FP8X4), scales=scales, in_=grouped)

        def quantize_k(codes, scales, k, grouped):
            quantize(codes[:, k, :], scales[:, k, :], grouped[:].rearrange("p r j -> p (r j)"))

        def tree(q):
            state = {"src": lt_sb[:, 2 * q : 2 * q + 2, :]}

            def level(lvl):
                half = 512 >> lvl
                m = rot.tile([P, 2, half], BF16, name="m%d" % lvl)
                src = state["src"]
                nc.vector.tensor_tensor(out=m[:], in0=src[:, :, 0:half], in1=src[:, :, half : 2 * half], op=ALU.max)
                state["src"] = m[:]

            def last():
                nc.vector.tensor_reduce(out=mx[:, 2 * q : 2 * q + 2], in_=state["src"], axis=AX.X, op=ALU.max)

            def negative():
                nc.vector.tensor_scalar(out=nmx[:, 2 * q : 2 * q + 2], in0=mx[:, 2 * q : 2 * q + 2], scalar1=-1.0, scalar2=None, op0=ALU.mult)

            return [lambda lvl=lvl: level(lvl) for lvl in range(5)] + [last, negative]

        def exps(q):
            for s in (2 * q, 2 * q + 1):
                g, t = divmod(s, 4)
                nc.scalar.activation(out=big[g][:, t, :], in_=lt_sb[:, s, :], func=ACT.Exp, bias=nmx[:, s : s + 1],
                                     scale=1.0, accum_out=rs[:, s : s + 1])

        def depth(q):
            def one(s):
                nc.vector.tensor_scalar(out=dd[:, s, :], in0=lt_sb[:, s, :], scalar1=nmx[:, s : s + 1], scalar2=None, op0=ALU.add)

            return [lambda s=s: one(s) for s in (2 * q, 2 * q + 1)]

        def guard_tree():
            def level(width):
                if width:
                    nc.vector.tensor_tensor(out=dd[:, 0:width, :], in0=dd[:, 0:width, :], in1=dd[:, width : 2 * width, :], op=ALU.max)

            return [lambda width=width: level(width) for width in (4, 2, 1)]

        tb = [scratch("tb%d" % g, [P, 4, N]) for g in range(2)]

        def deviation(q):
            g, tp = divmod(q, 2)
            s = slice(2 * q, 2 * q + 2)

            def inverse():
                nc.vector.reciprocal(out=rrs[:, s], in_=rs[:, s])

            def gain():
                nc.vector.scalar_tensor_tensor(out=amp[:, s], in0=rrs[:, s], scalar=float(N),
                                               in1=u_f[:, g, 2 * tp : 2 * tp + 2], op0=ALU.mult, op1=ALU.mult)

            def apply(t):
                nc.vector.tensor_scalar(out=tb[g][:, t, :], in0=big[g][:, t, :], scalar1=amp[:, 4 * g + t : 4 * g + t + 1],
                                        scalar2=u_f[:, g, t : t + 1], op0=ALU.mult, op1=ALU.subtract)

            return [inverse, gain] + [lambda t=t: apply(t) for t in (2 * tp, 2 * tp + 1)]

        t_int = {}

        def interleave_t(g, G, eng):
            if g not in t_int:
                t_int[g] = scratch("t_int", [P, N, 4])
            o = t_int[g][:, 512 * G : 512 * G + 512, :].rearrange("p (T q) t -> p T q t", T=4)
            i = tb[g][:, :, 512 * G : 512 * G + 512].rearrange("p t (q T) -> p T q t", T=4)
            if eng == "v":
                nc.vector.tensor_copy(out=o, in_=i)
            else:
                nc.scalar.copy(out=o, in_=i)

        def turn_in(rows, pr, kappa, dst, eng):
            dst_w = dst[:].rearrange("p r j -> p (r j)").bitcast(F32).rearrange("p (s r w) -> p s r w", s=8, w=2)
            bank = psum.tile([P, 2, 2, P], F32, name="tp", bufs=4)
            for s in range(2):
                words = rows[:, 2 * pr + s, :].bitcast(F32)
                for w in range(2):
                    nc.tensor.transpose(bank[:, s, w, :], words[:, 256 * kappa + w : 256 * kappa + 256 : 2], ident[:])
            o = dst_w[:, 2 * pr : 2 * pr + 2, :, :]
            i = bank[:].rearrange("p s w r -> p s r w")
            if eng == "v":
                nc.vector.tensor_copy(out=o, in_=i)
            else:
                nc.scalar.copy(out=o, in_=i)

        cv = {}
        jps = {}
        feat_t = {}
        ct = {}

        def first_product(i):
            cols = slice(P * i, P * i + P)
            for G in range(2):
                ctp = psum.tile([P, 4, P], F32, name="ctp", bufs=2)
                ct[i, G] = ctp
                for T in range(4):
                    mcols = slice(512 * G + P * T, 512 * G + P * T + P)
                    for k in range(2):
                        nc.tensor.matmul_mx(out=ctp[:, T, :], lhsT=t_codes[:, k, mcols].bitcast(FP8X4), lhsT_scale=t_scales[:, k, mcols],
                                            rhs=c1_codes[:, k, cols].bitcast(FP8X4), rhs_scale=c1_scales[:, k, cols],
                                            start=(k == 0), stop=(k == 1))

        def gain_cv(i, G):
            if G == 0:
                cv_int = rot.tile([P, 2, P, 4], BF16, name="cv_int", align_bytes=64, bufs=3)
                cv_codes = rot.tile([P, 2, P], U32, name="cv_codes", align_bytes=64, bufs=3)
                cv_scales = rot.tile([P, 2, P], U8, name="cv_scales", align_bytes=64, bufs=3)
                cv[i] = (cv_int, cv_codes, cv_scales)
            nc.vector.tensor_tensor(out=cv[i][0][:, G, :, :], in0=ct[i, G][:].rearrange("p T i -> p i T"),
                                    in1=v_f[:, G : G + 1, :].to_broadcast([P, P, 4]), op=ALU.mult)

        def quantize_cv(i):
            cv_int, cv_codes, cv_scales = cv[i]
            quantize(cv_codes[:].rearrange("p G i -> p (G i)"), cv_scales[:].rearrange("p G i -> p (G i)"),
                     cv_int[:].rearrange("p G i T -> p (G i T)"))

        def second_product(i):
            cv_int, cv_codes, cv_scales = cv[i]
            for h in range(2):
                hc = slice(512 * h, 512 * h + 512)
                jp = psum.tile([P, 512], F32, name="jp", bufs=2)
                jps[i, h] = jp
                for k in range(2):
                    nc.tensor.matmul_mx(out=jp[:], lhsT=cv_codes[:, k, :].bitcast(FP8X4), lhsT_scale=cv_scales[:, k, :],
                                        rhs=c2_codes[:, k, hc].bitcast(FP8X4), rhs_scale=c2_scales[:, k, hc],
                                        start=(k == 0), stop=(k == 1))

        def features(g, b):
            ft = psum.tile([P, 512], F32, name="tp", bufs=4)
            hc = slice(512 * g, 512 * g + 512)
            lcols = slice(P * b, P * b + P)
            nc.tensor.matmul_mx(out=ft[:], lhsT=y_codes[:, 0, lcols].bitcast(FP8X4), lhsT_scale=y_scales[:, 0, lcols],
                                rhs=x_codes[:, 0, hc].bitcast(FP8X4), rhs_scale=x_scales[:, 0, hc], start=True, stop=True)
            if g not in feat_t:
                feat_t[g] = keep.tile([P, 8, 512], F32, name="feat_t", tag="space%d" % g, align_bytes=64)
            dst = feat_t[g][:, b, :]
            if FEAT_ENG[8 * g + b] == "v":
                nc.vector.tensor_scalar(out=dst, in0=ft[:], scalar1=feat_scale, scalar2=lift_t[:, b : b + 1],
                                        op0=ALU.mult, op1=ALU.add)
            else:
                nc.scalar.activation(out=dst, in_=ft[:], func=ACT.Identity, scale=feat_scale, bias=lift_t[:, b : b + 1])

        def make_a(i):
            g, t = divmod(i, 4)
            banks = [psum.tile([P, 4, P], F32, name="tp", bufs=4) for h in range(2)]
            for h in range(2):
                nc.tensor.matmul(out=banks[h][:].rearrange("p b r -> p (b r)"), lhsT=ident_b[:], rhs=lt_sb[:, i, 512 * h : 512 * h + 512],
                                 start=True, stop=False)
            for h in range(2):
                for b in range(4):
                    nc.tensor.matmul(out=banks[h][:, b, :], lhsT=feat_t[g][:, 4 * h + b, P * t : P * t + P], rhs=ident[:],
                                     start=False, stop=(b == 3), is_transpose=True)
            for h in range(2):
                dst = big[g][:, t, 512 * h : 512 * h + 512]
                src = banks[h][:].rearrange("p b r -> p (b r)")
                if A_ENG[i] == "v":
                    nc.vector.tensor_copy(out=dst, in_=src)
                else:
                    nc.scalar.copy(out=dst, in_=src)

        def add_j(i, h):
            g, t = divmod(i, 4)
            hc = slice(512 * h, 512 * h + 512)
            nc.vector.scalar_tensor_tensor(out=big[g][:, t, hc], in0=jps[i, h][:], scalar=0.5, in1=big[g][:, t, hc],
                                           op0=ALU.mult, op1=ALU.add)

        def row_max(i):
            g, t = divmod(i, 4)
            nc.vector.tensor_reduce(out=rmax[:, i : i + 1], in_=big[g][:, t, :], axis=AX.X, op=ALU.max)

        def row_shift(i):
            nc.vector.tensor_scalar(out=nrmax[:, i : i + 1], in0=rmax[:, i : i + 1], scalar1=-1.0, scalar2=LIFT, op0=ALU.mult, op1=ALU.add)

        def row_exp(i):
            g, t = divmod(i, 4)
            nc.scalar.activation(out=big[g][:, t, :], in_=big[g][:, t, :], func=ACT.Exp, bias=nrmax[:, i : i + 1], scale=1.0,
                                 accum_out=rs2[:, i : i + 1])

        def weight(i):
            def inverse():
                nc.vector.reciprocal(out=w1[:, i : i + 1], in_=rs2[:, i : i + 1])

            def scaled():
                nc.vector.tensor_scalar(out=w2[:, i : i + 1], in0=w1[:, i : i + 1], scalar1=W_SCALE, scalar2=None, op0=ALU.mult)

            return [inverse, scaled]

        css = {}

        def column_part(slots):
            cs = psum.tile([P, 8], F32, name="tp", bufs=4)
            css[slots] = cs
            for b in range(8):
                for s in slots:
                    nc.tensor.matmul(out=cs[:, b : b + 1], lhsT=big[s // 4][:, s % 4, P * b : P * b + P], rhs=w2[:, s : s + 1],
                                     start=(s == slots[0]), stop=(s == slots[-1]))

        def column_add(slots):
            if slots[0] == 0:
                nc.vector.tensor_scalar(out=csum[:], in0=css[slots][:], scalar1=1.0 / N, scalar2=None, op0=ALU.mult)
            else:
                nc.vector.scalar_tensor_tensor(out=csum[:], in0=css[slots][:], scalar=1.0 / N, in1=csum[:], op0=ALU.mult, op1=ALU.add)

        dT = {}

        def guard_turn():
            dT[0] = psum.tile([P, 8, P], BF16, name="tp", bufs=4)
            for b in range(8):
                nc.tensor.transpose(dT[0][:, b, :], dd[:, 0, P * b : P * b + P], ident_b[:])

        def guard_end():
            def deepest():
                nc.vector.tensor_reduce(out=hT[:], in_=dT[0][:], axis=AX.X, op=ALU.max)

            def cut():
                nc.vector.tensor_scalar(out=hG[:], in0=hT[:], scalar1=DEEP, scalar2=0.0, op0=ALU.add, op1=ALU.min)

            def sign():
                nc.vector.tensor_scalar(out=lift_t[:], in0=hG[:], scalar1=-1.0, scalar2=None, op0=ALU.mult)

            return [deepest, cut, sign]

        def spread(c, half):
            bank = psum.tile([P, 4, P], F32, name="tp", bufs=4)
            for b in range(4):
                nc.tensor.transpose(bank[:, b, :], c[:, 4 * half + b : 4 * half + b + 1].to_broadcast([P, P]), ident[:])
            return bank

        def widen_u():
            nc.vector.tensor_copy(out=u_f[:], in_=u_raw[:])

        def widen_v():
            nc.vector.tensor_copy(out=v_f[:], in_=v_raw[:])

        weave(tree(0))
        exps(0)
        weave(tree(1), [widen_u, widen_v] + depth(0))
        exps(1)
        weave(tree(2), tree(3), depth(1))
        exps(2)
        exps(3)
        c1_g = [scratch("c1_int", [P, N, 4]) for k in range(2)]

        def turn_c1(half):
            for k in range(2):
                for pr in (2 * half, 2 * half + 1):
                    turn_in(c1_sb, pr, k, c1_g[k], C1_ENG[4 * half + 2 * k + pr % 2])

        weave(deviation(0), depth(2))
        weave(deviation(1), depth(3))
        turn_c1(0)
        gt = guard_tree()
        gt[0]()
        interleave_t(0, 0, "v")
        weave(deviation(2), gt[1:])
        weave(deviation(3))
        interleave_t(0, 1, "s")
        interleave_t(1, 1, "s")
        turn_c1(1)
        guard_turn()
        interleave_t(1, 0, "v")
        quantize_k(t_codes, t_scales, 0, t_int[0])
        ge = guard_end()
        ge[0]()
        quantize_k(t_codes, t_scales, 1, t_int[1])
        ge[1]()
        x_g = scratch("x_int", [P, N, 4])
        y_g = scratch("y_int", [P, N, 4])
        for pr in range(4):
            turn_in(xy_sb[:, 0, :, :], pr, 0, x_g, X_ENG[pr])
        for pr in range(4):
            turn_in(xy_sb[:, 1, :, :], pr, 0, y_g, Y_ENG[pr])
        quantize_k(c1_codes, c1_scales, 0, c1_g[0])
        ge[2]()
        quantize_k(c1_codes, c1_scales, 1, c1_g[1])
        first_product(0)
        quantize_k(x_codes, x_scales, 0, x_g)
        gain_cv(0, 0)
        gain_cv(0, 1)
        quantize_k(y_codes, y_scales, 0, y_g)
        c2_g = [scratch("c2_int", [P, N, 4]) for k in range(2)]
        for n in range(4):
            turn_in(c2_sb, n, 0, c2_g[0], C2_ENG[n])
        quantize_cv(0)
        first_product(1)
        for b in range(4):
            features(0, b)
        gain_cv(1, 0)
        gain_cv(1, 1)
        quantize_k(c2_codes, c2_scales, 0, c2_g[0])
        for n in range(4):
            turn_in(c2_sb, n, 1, c2_g[1], C2_ENG[4 + n])
        for b in range(4, 8):
            features(0, b)
        quantize_cv(1)
        first_product(2)
        make_a(0)
        quantize_k(c2_codes, c2_scales, 1, c2_g[1])
        make_a(1)
        for i in range(8):
            second_product(i)
            if i < 6:
                gain_cv(i + 2, 0)
                gain_cv(i + 2, 1)
            if i < 5:
                first_product(i + 3)
            if i < 2:
                for b in range(4 * i, 4 * i + 4):
                    features(1, b)
            if i in (3, 5, 7):
                column_part((i - 3, i - 2))
            if i < 6:
                make_a(i + 2)
            add_j(i, 0)
            add_j(i, 1)
            if i < 6:
                quantize_cv(i + 2)
            row_max(i)
            w = weight(i - 1) if i > 0 else [None, None]
            if i > 0:
                w[0]()
            row_shift(i)
            row_exp(i)
            if i > 0:
                w[1]()
            if i in (3, 5, 7):
                column_add((i - 3, i - 2))
        column_part((6,))
        weave(weight(7))
        column_part((7,))
        column_add((6,))
        column_add((7,))

        nc.vector.reciprocal(out=rc1[:], in_=csum[:])
        RC = [spread(rc1, h) for h in range(2)]
        o_int = {}

        def scale_out(g, h):
            hc = slice(512 * h, 512 * h + 512)
            for t in range(4):
                i = 4 * g + t
                nc.vector.scalar_tensor_tensor(out=big[g][:, t, hc], in0=big[g][:, t, hc], scalar=w2[:, i : i + 1],
                                               in1=RC[h][:].rearrange("p b r -> p (b r)"), op0=ALU.mult, op1=ALU.mult)
            nc.sync.dma_start(out=out_0[512 * g : 512 * g + 512, hc].rearrange("(p t) m -> p t m", t=4), in_=big[g][:, :, hc])
            o_int[g, h] = scratch("o_int", [P, 512, 4])

        def interleave_out(g, h, split):
            for a, b, eng in split:
                src = big[g][:, :, 512 * h + a : 512 * h + b].rearrange("p t m -> p m t")
                if eng == "s":
                    nc.scalar.copy(out=o_int[g, h][:, a:b, :], in_=src)
                else:
                    nc.vector.tensor_copy(out=o_int[g, h][:, a:b, :], in_=src)

        def quantize_out(g, h):
            hc = slice(512 * h, 512 * h + 512)
            quantize(o_codes[:, g, hc], o_scales[:, g, hc], o_int[g, h][:].rearrange("p m t -> p (m t)"))
            nc.sync.dma_start(out=out_1[g, :, hc, :].rearrange("p m t -> p (m t)").bitcast(I32), in_=o_codes[:, g, hc].bitcast(I32))

        scale_out(0, 0)
        interleave_out(0, 0, ((0, 512, "s"),))
        scale_out(0, 1)
        interleave_out(0, 1, ((0, 512, "s"),))
        quantize_out(0, 0)
        scale_out(1, 0)
        interleave_out(1, 0, ((0, 256, "s"), (256, 512, "v")))
        quantize_out(0, 1)
        scale_out(1, 1)
        quantize_out(1, 0)
        interleave_out(1, 1, ((0, 192, "s"), (192, 512, "v")))
        quantize_out(1, 1)
        for Q in range(4):
            nc.sync.dma_start(out=out_2[:, 4 * Q : 4 * Q + 4, :].rearrange("g r m -> r g m").bitcast(I32),
                              in_=o_scales[32 * Q : 32 * Q + 4, :, :].bitcast(I32))
